import numpy as np
import ml_dtypes

BF16 = ml_dtypes.bfloat16


def bf(x):
    return np.asarray(x, np.float32).astype(BF16)


def f32(x):
    return np.asarray(x, np.float32)


def f64(x):
    return np.asarray(x).astype(np.float64)


def striped(idx):
    return np.tile(idx.reshape(-1, 16).T, (8, 1))


S, K, H, M, N, E, Q = 512, 512, 256, 128, 512, 1, 512


def setup_inputs():
    return {"base": bf(np.random.standard_normal((M, S))), "x": bf(np.random.standard_normal((K, N))), "w": bf(np.random.standard_normal((E, K, H)) / np.sqrt(K)), "b": f32(0.5 * np.random.standard_normal((H, E))), "w2": bf(1.5 * np.random.standard_normal((E, H, M)) / np.sqrt(H)), "c": f32(0.2 + 0.8 * np.random.random_sample((1, N))), "offs": striped(np.random.permutation(S))}


def reference(base, x, w, b, w2, c, offs):
    idx = offs[:16].T.reshape(-1)
    z = f64(base).copy()
    for e in range(E):
        t = f64(w)[e].T @ f64(x)[:, e * Q : (e + 1) * Q] + f64(b)[:, e : e + 1]
        t = np.maximum(t, 0.0) * f64(c)[:, e * Q : (e + 1) * Q]
        z[:, idx[e * Q : (e + 1) * Q]] += f64(w2)[e].T @ t
    return z

@@ -1,0 +1,62 @@
+import concourse.mybir as mybir
+from concourse.masks import make_identity
+
+P = 128
+N = 512
+K = 512
+H = 256
+KB = K // P
+HB = H // P
+
+FLOPS = 2 * K * H * N + 2 * H * P * N
+
+BF16, F32, U16 = mybir.dt.bfloat16, mybir.dt.float32, mybir.dt.uint16
+RELU = mybir.ActivationFunctionType.Relu
+MULT = mybir.AluOpType.mult
+
+
+def tile_rows_ffnback_relu_kernel(tc, base, x, w, b, w2, c, offs, out):
+    nc = tc.nc
+    with (
+        tc.tile_pool(name="held", bufs=1) as held,
+        tc.psum_pool(name="psum", bufs=1) as psum,
+    ):
+        w_sb = held.tile([P, KB, H], BF16)
+        x_sb = held.tile([P, KB, N], BF16)
+        base_sb = held.tile([P, N], BF16)
+        w2_sb = held.tile([P, HB, P], BF16)
+        offsets = held.tile([P, N // 16], U16)
+        b_sb = held.tile([P, HB], F32)
+        c_sb = held.tile([P, N], F32)
+        x_rows = x.rearrange("(p a) n -> p a n", p=P)
+        nc.sync.dma_start(w_sb[:], w[0].rearrange("(p a) h -> p a h", p=P))
+        nc.sync.dma_start(x_sb[:, 0 : KB // 2, :], x_rows[:, 0 : KB // 2, :])
+        nc.sync.dma_start(x_sb[:, KB // 2 : KB, :], x_rows[:, KB // 2 : KB, :])
+        nc.sync.dma_start(base_sb[:], base)
+        nc.sync.dma_start(w2_sb[:], w2[0].rearrange("(a p) m -> p a m", p=P))
+        nc.sync.dma_start(offsets[:], offs)
+        nc.scalar.dma_start(b_sb[:], b.rearrange("(a p) o -> p (a o)", p=P))
+        nc.scalar.dma_start(c_sb[:], c.rearrange("o n -> (o n)").partition_broadcast(P))
+
+        ident = held.tile([P, P], BF16)
+        make_identity(nc, ident[:])
+        window = psum.tile([P, N], F32)
+
+        layer1 = [psum.tile([P, N], F32, name=f"layer1_{a}") for a in range(HB)]
+        for k in range(KB):
+            for a in range(HB):
+                nc.tensor.matmul(
+                    layer1[a][:], w_sb[:, k, a * P : (a + 1) * P], x_sb[:, k, :], start=k == 0, stop=k == KB - 1
+                )
+        nc.tensor.matmul(window[:], ident[:], base_sb[:], start=True, stop=False)
+
+        for a in range(HB):
+            relu = held.tile([P, N], F32, name=f"relu_{a}")
+            nc.scalar.activation(relu[:], layer1[a][:], RELU, bias=b_sb[:, a : a + 1])
+            h = held.tile([P, N], BF16, name=f"h_{a}")
+            nc.vector.tensor_tensor(h[:], relu[:], c_sb[:], MULT)
+            nc.tensor.matmul(window[:].indirect(offsets[:]), w2_sb[:, a, :], h[:], start=False, stop=a == HB - 1)
+
+        out_sb = held.tile([P, N], F32)
+        nc.vector.tensor_copy(out_sb[:], window[:])
+        nc.sync.dma_start(out, out_sb[:])

@@ -11,8 +11,9 @@ HB = H // P
 FLOPS = 2 * K * H * N + 2 * H * P * N
 
 BF16, F32, U16 = mybir.dt.bfloat16, mybir.dt.float32, mybir.dt.uint16
-RELU = mybir.ActivationFunctionType.Relu
-MULT = mybir.AluOpType.mult
+WARM_UPS = 3
+
+MAX, MULT, SUBTRACT = mybir.AluOpType.max, mybir.AluOpType.mult, mybir.AluOpType.subtract
 
 
 def tile_rows_ffnback_relu_kernel(tc, base, x, w, b, w2, c, offs, out):
@@ -26,35 +27,51 @@ def tile_rows_ffnback_relu_kernel(tc, base, x, w, b, w2, c, offs, out):
         base_sb = held.tile([P, N], BF16)
         w2_sb = held.tile([P, HB, P], BF16)
         offsets = held.tile([P, N // 16], U16)
-        b_sb = held.tile([P, HB], F32)
+        b_row = held.tile([1, H], F32)
         c_sb = held.tile([P, N], F32)
         x_rows = x.rearrange("(p a) n -> p a n", p=P)
+        nc.sync.dma_start(b_row[:], b.rearrange("h o -> o h"))
         nc.sync.dma_start(w_sb[:], w[0].rearrange("(p a) h -> p a h", p=P))
         nc.sync.dma_start(x_sb[:, 0 : KB // 2, :], x_rows[:, 0 : KB // 2, :])
         nc.sync.dma_start(x_sb[:, KB // 2 : KB, :], x_rows[:, KB // 2 : KB, :])
         nc.sync.dma_start(base_sb[:], base)
         nc.sync.dma_start(w2_sb[:], w2[0].rearrange("(a p) m -> p a m", p=P))
         nc.sync.dma_start(offsets[:], offs)
-        nc.scalar.dma_start(b_sb[:], b.rearrange("(a p) o -> p (a o)", p=P))
         nc.scalar.dma_start(c_sb[:], c.rearrange("o n -> (o n)").partition_broadcast(P))
+
+        zeros = held.tile([P, N], BF16)
+        nc.vector.memset(zeros[:], 0.0)
+        ones_row = held.tile([1, N], BF16)
+        nc.vector.memset(ones_row[:], 1.0)
+        warm = psum.tile([P, N], F32)
+        for i in range(WARM_UPS):
+            nc.tensor.matmul(warm[:], zeros[:, 0:P], zeros[:], start=True, stop=True)
 
         ident = held.tile([P, P], BF16)
         make_identity(nc, ident[:])
-        window = psum.tile([P, N], F32)
+
+        b_high = held.tile([1, H], BF16)
+        b_low = held.tile([1, H], BF16)
+        nc.vector.tensor_copy(b_high[:], b_row[:])
+        nc.vector.tensor_tensor(b_low[:], b_row[:], b_high[:], SUBTRACT)
 
         layer1 = [psum.tile([P, N], F32, name=f"layer1_{a}") for a in range(HB)]
-        for k in range(KB):
+        for a in range(HB):
+            nc.tensor.matmul(layer1[a][:], b_high[:, a * P : (a + 1) * P], ones_row[:], start=True, stop=False)
+            nc.tensor.matmul(layer1[a][:], b_low[:, a * P : (a + 1) * P], ones_row[:], start=False, stop=False)
+        for half in range(2):
             for a in range(HB):
-                nc.tensor.matmul(
-                    layer1[a][:], w_sb[:, k, a * P : (a + 1) * P], x_sb[:, k, :], start=k == 0, stop=k == KB - 1
-                )
+                for k in range(half * KB // 2, (half + 1) * KB // 2):
+                    nc.tensor.matmul(
+                        layer1[a][:], w_sb[:, k, a * P : (a + 1) * P], x_sb[:, k, :], start=False, stop=k == KB - 1
+                    )
+
+        window = psum.tile([P, N], F32)
         nc.tensor.matmul(window[:], ident[:], base_sb[:], start=True, stop=False)
 
         for a in range(HB):
-            relu = held.tile([P, N], F32, name=f"relu_{a}")
-            nc.scalar.activation(relu[:], layer1[a][:], RELU, bias=b_sb[:, a : a + 1])
             h = held.tile([P, N], BF16, name=f"h_{a}")
-            nc.vector.tensor_tensor(h[:], relu[:], c_sb[:], MULT)
+            nc.vector.scalar_tensor_tensor(h[:], layer1[a][:], 0.0, c_sb[:], MAX, MULT)
             nc.tensor.matmul(window[:].indirect(offsets[:]), w2_sb[:, a, :], h[:], start=False, stop=a == HB - 1)
 
         out_sb = held.tile([P, N], F32)

@@ -7,13 +7,14 @@ K = 512
 H = 256
 KB = K // P
 HB = H // P
+PIECE = 256
+WARM_UPS = 4
 
 FLOPS = 2 * K * H * N + 2 * H * P * N
 
 BF16, F32, U16 = mybir.dt.bfloat16, mybir.dt.float32, mybir.dt.uint16
-WARM_UPS = 3
-
-MAX, MULT, SUBTRACT = mybir.AluOpType.max, mybir.AluOpType.mult, mybir.AluOpType.subtract
+RELU = mybir.ActivationFunctionType.Relu
+MULT = mybir.AluOpType.mult
 
 
 def tile_rows_ffnback_relu_kernel(tc, base, x, w, b, w2, c, offs, out):
@@ -27,52 +28,55 @@ def tile_rows_ffnback_relu_kernel(tc, base, x, w, b, w2, c, offs, out):
         base_sb = held.tile([P, N], BF16)
         w2_sb = held.tile([P, HB, P], BF16)
         offsets = held.tile([P, N // 16], U16)
-        b_row = held.tile([1, H], F32)
+        b_sb = held.tile([P, HB], F32)
         c_sb = held.tile([P, N], F32)
         x_rows = x.rearrange("(p a) n -> p a n", p=P)
-        nc.sync.dma_start(b_row[:], b.rearrange("h o -> o h"))
         nc.sync.dma_start(w_sb[:], w[0].rearrange("(p a) h -> p a h", p=P))
         nc.sync.dma_start(x_sb[:, 0 : KB // 2, :], x_rows[:, 0 : KB // 2, :])
         nc.sync.dma_start(x_sb[:, KB // 2 : KB, :], x_rows[:, KB // 2 : KB, :])
         nc.sync.dma_start(base_sb[:], base)
         nc.sync.dma_start(w2_sb[:], w2[0].rearrange("(a p) m -> p a m", p=P))
         nc.sync.dma_start(offsets[:], offs)
-        nc.scalar.dma_start(c_sb[:], c.rearrange("o n -> (o n)").partition_broadcast(P))
+        nc.sync.dma_start(c_sb[:], c.rearrange("o n -> (o n)").partition_broadcast(P))
+        nc.scalar.dma_start(b_sb[:], b.rearrange("(a p) o -> p (a o)", p=P))
 
         zeros = held.tile([P, N], BF16)
         nc.vector.memset(zeros[:], 0.0)
-        ones_row = held.tile([1, N], BF16)
-        nc.vector.memset(ones_row[:], 1.0)
         warm = psum.tile([P, N], F32)
         for i in range(WARM_UPS):
             nc.tensor.matmul(warm[:], zeros[:, 0:P], zeros[:], start=True, stop=True)
 
+        early = held.tile([P, 1], F32)
+        nc.scalar.activation(early[:], zeros[:, 0:1], RELU)
+
         ident = held.tile([P, P], BF16)
         make_identity(nc, ident[:])
 
-        b_high = held.tile([1, H], BF16)
-        b_low = held.tile([1, H], BF16)
-        nc.vector.tensor_copy(b_high[:], b_row[:])
-        nc.vector.tensor_tensor(b_low[:], b_row[:], b_high[:], SUBTRACT)
-
         layer1 = [psum.tile([P, N], F32, name=f"layer1_{a}") for a in range(HB)]
-        for a in range(HB):
-            nc.tensor.matmul(layer1[a][:], b_high[:, a * P : (a + 1) * P], ones_row[:], start=True, stop=False)
-            nc.tensor.matmul(layer1[a][:], b_low[:, a * P : (a + 1) * P], ones_row[:], start=False, stop=False)
         for half in range(2):
             for a in range(HB):
                 for k in range(half * KB // 2, (half + 1) * KB // 2):
                     nc.tensor.matmul(
-                        layer1[a][:], w_sb[:, k, a * P : (a + 1) * P], x_sb[:, k, :], start=False, stop=k == KB - 1
+                        layer1[a][:], w_sb[:, k, a * P : (a + 1) * P], x_sb[:, k, :], start=k == 0, stop=k == KB - 1
                     )
 
         window = psum.tile([P, N], F32)
         nc.tensor.matmul(window[:], ident[:], base_sb[:], start=True, stop=False)
 
         for a in range(HB):
-            h = held.tile([P, N], BF16, name=f"h_{a}")
-            nc.vector.scalar_tensor_tensor(h[:], layer1[a][:], 0.0, c_sb[:], MAX, MULT)
-            nc.tensor.matmul(window[:].indirect(offsets[:]), w2_sb[:, a, :], h[:], start=False, stop=a == HB - 1)
+            for first in range(0, N, PIECE):
+                entries = slice(first, first + PIECE)
+                relu = held.tile([P, PIECE], F32, name=f"relu_{a}_{first}")
+                nc.scalar.activation(relu[:], layer1[a][:, entries], RELU, bias=b_sb[:, a : a + 1])
+                h = held.tile([P, PIECE], BF16, name=f"h_{a}_{first}")
+                nc.vector.tensor_tensor(h[:], relu[:], c_sb[:, entries], MULT)
+                nc.tensor.matmul(
+                    window[:].indirect(offsets[:, first // 16 : (first + PIECE) // 16]),
+                    w2_sb[:, a, :],
+                    h[:],
+                    start=False,
+                    stop=a == HB - 1 and first + PIECE == N,
+                )
 
         out_sb = held.tile([P, N], F32)
         nc.vector.tensor_copy(out_sb[:], window[:])

@@ -8,13 +8,14 @@ H = 256
 KB = K // P
 HB = H // P
 PIECE = 256
+LOW = 32
 WARM_UPS = 4
 
 FLOPS = 2 * K * H * N + 2 * H * P * N
 
 BF16, F32, U16 = mybir.dt.bfloat16, mybir.dt.float32, mybir.dt.uint16
 RELU = mybir.ActivationFunctionType.Relu
-MULT = mybir.AluOpType.mult
+MULT, SUBTRACT = mybir.AluOpType.mult, mybir.AluOpType.subtract
 
 
 def tile_rows_ffnback_relu_kernel(tc, base, x, w, b, w2, c, offs, out):
@@ -29,7 +30,7 @@ def tile_rows_ffnback_relu_kernel(tc, base, x, w, b, w2, c, offs, out):
         w2_sb = held.tile([P, HB, P], BF16)
         offsets = held.tile([P, N // 16], U16)
         b_sb = held.tile([P, HB], F32)
-        c_sb = held.tile([P, N], F32)
+        c_rows = held.tile([LOW + 1, N], F32)
         x_rows = x.rearrange("(p a) n -> p a n", p=P)
         nc.sync.dma_start(w_sb[:], w[0].rearrange("(p a) h -> p a h", p=P))
         nc.sync.dma_start(x_sb[:, 0 : KB // 2, :], x_rows[:, 0 : KB // 2, :])
@@ -37,7 +38,7 @@ def tile_rows_ffnback_relu_kernel(tc, base, x, w, b, w2, c, offs, out):
         nc.sync.dma_start(base_sb[:], base)
         nc.sync.dma_start(w2_sb[:], w2[0].rearrange("(a p) m -> p a m", p=P))
         nc.sync.dma_start(offsets[:], offs)
-        nc.sync.dma_start(c_sb[:], c.rearrange("o n -> (o n)").partition_broadcast(P))
+        nc.scalar.dma_start(c_rows[0 : LOW + 1 : LOW, :], c.rearrange("o n -> (o n)").partition_broadcast(2))
         nc.scalar.dma_start(b_sb[:], b.rearrange("(a p) o -> p (a o)", p=P))
 
         zeros = held.tile([P, N], BF16)
@@ -45,6 +46,16 @@ def tile_rows_ffnback_relu_kernel(tc, base, x, w, b, w2, c, offs, out):
         warm = psum.tile([P, N], F32)
         for i in range(WARM_UPS):
             nc.tensor.matmul(warm[:], zeros[:, 0:P], zeros[:], start=True, stop=True)
+
+        c_parts = held.tile([P, N], BF16)
+        nc.gpsimd.memset(c_parts[:], 0.0)
+        c_rounded = held.tile([LOW + 1, N], BF16)
+        low = slice(LOW, LOW + 1)
+        nc.vector.tensor_copy(c_rounded[low, :], c_rows[low, :])
+        nc.vector.tensor_tensor(c_parts[low, :], c_rows[low, :], c_rounded[low, :], SUBTRACT)
+        nc.vector.tensor_copy(c_parts[0:1, :], c_rows[0:1, :])
+        ones = held.tile([P, P], BF16)
+        nc.vector.memset(ones[:], 1.0)
 
         early = held.tile([P, 1], F32)
         nc.scalar.activation(early[:], zeros[:, 0:1], RELU)
@@ -59,6 +70,9 @@ def tile_rows_ffnback_relu_kernel(tc, base, x, w, b, w2, c, offs, out):
                     nc.tensor.matmul(
                         layer1[a][:], w_sb[:, k, a * P : (a + 1) * P], x_sb[:, k, :], start=k == 0, stop=k == KB - 1
                     )
+            if half == 0:
+                spread = psum.tile([P, N], F32)
+                nc.tensor.matmul(spread[:], ones[:], c_parts[:], start=True, stop=True)
 
         window = psum.tile([P, N], F32)
         nc.tensor.matmul(window[:], ident[:], base_sb[:], start=True, stop=False)
@@ -69,7 +83,7 @@ def tile_rows_ffnback_relu_kernel(tc, base, x, w, b, w2, c, offs, out):
                 relu = held.tile([P, PIECE], F32, name=f"relu_{a}_{first}")
                 nc.scalar.activation(relu[:], layer1[a][:, entries], RELU, bias=b_sb[:, a : a + 1])
                 h = held.tile([P, PIECE], BF16, name=f"h_{a}_{first}")
-                nc.vector.tensor_tensor(h[:], relu[:], c_sb[:, entries], MULT)
+                nc.vector.tensor_tensor(h[:], relu[:], spread[:, entries], MULT)
                 nc.tensor.matmul(
                     window[:].indirect(offsets[:, first // 16 : (first + PIECE) // 16]),
                     w2_sb[:, a, :],

@@ -8,8 +8,9 @@ H = 256
 KB = K // P
 HB = H // P
 PIECE = 256
+PIECES = range(0, N, PIECE)
 LOW = 32
-WARM_UPS = 4
+WARM_UPS = 3
 
 FLOPS = 2 * K * H * N + 2 * H * P * N
 
@@ -32,9 +33,10 @@ def tile_rows_ffnback_relu_kernel(tc, base, x, w, b, w2, c, offs, out):
         b_sb = held.tile([P, HB], F32)
         c_rows = held.tile([LOW + 1, N], F32)
         x_rows = x.rearrange("(p a) n -> p a n", p=P)
-        nc.sync.dma_start(w_sb[:], w[0].rearrange("(p a) h -> p a h", p=P))
-        nc.sync.dma_start(x_sb[:, 0 : KB // 2, :], x_rows[:, 0 : KB // 2, :])
-        nc.sync.dma_start(x_sb[:, KB // 2 : KB, :], x_rows[:, KB // 2 : KB, :])
+        w_rows = w[0].rearrange("(p a) h -> p a h", p=P)
+        for half in (slice(0, KB // 2), slice(KB // 2, KB)):
+            nc.sync.dma_start(w_sb[:, half, :], w_rows[:, half, :])
+            nc.sync.dma_start(x_sb[:, half, :], x_rows[:, half, :])
         nc.sync.dma_start(base_sb[:], base)
         nc.sync.dma_start(w2_sb[:], w2[0].rearrange("(a p) m -> p a m", p=P))
         nc.sync.dma_start(offsets[:], offs)
@@ -63,13 +65,20 @@ def tile_rows_ffnback_relu_kernel(tc, base, x, w, b, w2, c, offs, out):
         ident = held.tile([P, P], BF16)
         make_identity(nc, ident[:])
 
-        layer1 = [psum.tile([P, N], F32, name=f"layer1_{a}") for a in range(HB)]
+        layer1 = {
+            (a, first): psum.tile([P, PIECE], F32, name=f"layer1_{a}_{first}") for a in range(HB) for first in PIECES
+        }
         for half in range(2):
             for a in range(HB):
-                for k in range(half * KB // 2, (half + 1) * KB // 2):
-                    nc.tensor.matmul(
-                        layer1[a][:], w_sb[:, k, a * P : (a + 1) * P], x_sb[:, k, :], start=k == 0, stop=k == KB - 1
-                    )
+                for first in PIECES:
+                    for k in range(half * KB // 2, (half + 1) * KB // 2):
+                        nc.tensor.matmul(
+                            layer1[a, first][:],
+                            w_sb[:, k, a * P : (a + 1) * P],
+                            x_sb[:, k, first : first + PIECE],
+                            start=k == 0,
+                            stop=k == KB - 1,
+                        )
             if half == 0:
                 spread = psum.tile([P, N], F32)
                 nc.tensor.matmul(spread[:], ones[:], c_parts[:], start=True, stop=True)
@@ -78,12 +87,11 @@ def tile_rows_ffnback_relu_kernel(tc, base, x, w, b, w2, c, offs, out):
         nc.tensor.matmul(window[:], ident[:], base_sb[:], start=True, stop=False)
 
         for a in range(HB):
-            for first in range(0, N, PIECE):
-                entries = slice(first, first + PIECE)
+            for first in PIECES:
                 relu = held.tile([P, PIECE], F32, name=f"relu_{a}_{first}")
-                nc.scalar.activation(relu[:], layer1[a][:, entries], RELU, bias=b_sb[:, a : a + 1])
+                nc.scalar.activation(relu[:], layer1[a, first][:], RELU, bias=b_sb[:, a : a + 1])
                 h = held.tile([P, PIECE], BF16, name=f"h_{a}_{first}")
-                nc.vector.tensor_tensor(h[:], relu[:], spread[:, entries], MULT)
+                nc.vector.tensor_tensor(h[:], relu[:], spread[:, first : first + PIECE], MULT)
                 nc.tensor.matmul(
                     window[:].indirect(offsets[:, first // 16 : (first + PIECE) // 16]),
                     w2_sb[:, a, :],
@@ -92,6 +100,7 @@ def tile_rows_ffnback_relu_kernel(tc, base, x, w, b, w2, c, offs, out):
                     stop=a == HB - 1 and first + PIECE == N,
                 )
 
-        out_sb = held.tile([P, N], F32)
-        nc.vector.tensor_copy(out_sb[:], window[:])
-        nc.sync.dma_start(out, out_sb[:])
+        for first in PIECES:
+            out_sb = held.tile([P, PIECE], F32, name=f"out_{first}")
+            nc.vector.tensor_copy(out_sb[:], window[:, first : first + PIECE])
+            nc.sync.dma_start(out[:, first : first + PIECE], out_sb[:])

import concourse.mybir as mybir
from concourse.masks import make_identity

P = 128
N = 512
K = 512
H = 256
KB = K // P
HB = H // P
PIECE = 256
PIECES = range(0, N, PIECE)
LOW = 32
WARM_UPS = 3

FLOPS = 2 * K * H * N + 2 * H * P * N

BF16, F32, U16 = mybir.dt.bfloat16, mybir.dt.float32, mybir.dt.uint16
RELU = mybir.ActivationFunctionType.Relu
MULT, SUBTRACT = mybir.AluOpType.mult, mybir.AluOpType.subtract


def tile_rows_ffnback_relu_kernel(tc, base, x, w, b, w2, c, offs, out):
    nc = tc.nc
    with (
        tc.tile_pool(name="held", bufs=1) as held,
        tc.psum_pool(name="psum", bufs=1) as psum,
    ):
        w_sb = held.tile([P, KB, H], BF16)
        x_sb = held.tile([P, KB, N], BF16)
        base_sb = held.tile([P, N], BF16)
        w2_sb = held.tile([P, HB, P], BF16)
        offsets = held.tile([P, N // 16], U16)
        b_sb = held.tile([P, HB], F32)
        c_rows = held.tile([LOW + 1, N], F32)
        x_rows = x.rearrange("(p a) n -> p a n", p=P)
        w_rows = w[0].rearrange("(p a) h -> p a h", p=P)
        for half in (slice(0, KB // 2), slice(KB // 2, KB)):
            nc.sync.dma_start(w_sb[:, half, :], w_rows[:, half, :])
            nc.sync.dma_start(x_sb[:, half, :], x_rows[:, half, :])
        nc.sync.dma_start(base_sb[:], base)
        nc.sync.dma_start(w2_sb[:], w2[0].rearrange("(a p) m -> p a m", p=P))
        nc.sync.dma_start(offsets[:], offs)
        nc.scalar.dma_start(c_rows[0 : LOW + 1 : LOW, :], c.rearrange("o n -> (o n)").partition_broadcast(2))
        nc.scalar.dma_start(b_sb[:], b.rearrange("(a p) o -> p (a o)", p=P))

        zeros = held.tile([P, N], BF16)
        nc.vector.memset(zeros[:], 0.0)
        warm = psum.tile([P, N], F32)
        for i in range(WARM_UPS):
            nc.tensor.matmul(warm[:], zeros[:, 0:P], zeros[:], start=True, stop=True)

        c_parts = held.tile([P, N], BF16)
        nc.gpsimd.memset(c_parts[:], 0.0)
        c_rounded = held.tile([LOW + 1, N], BF16)
        low = slice(LOW, LOW + 1)
        nc.vector.tensor_copy(c_rounded[low, :], c_rows[low, :])
        nc.vector.tensor_tensor(c_parts[low, :], c_rows[low, :], c_rounded[low, :], SUBTRACT)
        nc.vector.tensor_copy(c_parts[0:1, :], c_rows[0:1, :])
        ones = held.tile([P, P], BF16)
        nc.vector.memset(ones[:], 1.0)

        early = held.tile([P, 1], F32)
        nc.scalar.activation(early[:], zeros[:, 0:1], RELU)

        ident = held.tile([P, P], BF16)
        make_identity(nc, ident[:])

        layer1 = {
            (a, first): psum.tile([P, PIECE], F32, name=f"layer1_{a}_{first}") for a in range(HB) for first in PIECES
        }
        for half in range(2):
            for a in range(HB):
                for first in PIECES:
                    for k in range(half * KB // 2, (half + 1) * KB // 2):
                        nc.tensor.matmul(
                            layer1[a, first][:],
                            w_sb[:, k, a * P : (a + 1) * P],
                            x_sb[:, k, first : first + PIECE],
                            start=k == 0,
                            stop=k == KB - 1,
                        )
            if half == 0:
                spread = psum.tile([P, N], F32)
                nc.tensor.matmul(spread[:], ones[:], c_parts[:], start=True, stop=True)

        window = psum.tile([P, N], F32)
        nc.tensor.matmul(window[:], ident[:], base_sb[:], start=True, stop=False)

        for a in range(HB):
            for first in PIECES:
                relu = held.tile([P, PIECE], F32, name=f"relu_{a}_{first}")
                nc.scalar.activation(relu[:], layer1[a, first][:], RELU, bias=b_sb[:, a : a + 1])
                h = held.tile([P, PIECE], BF16, name=f"h_{a}_{first}")
                nc.vector.tensor_tensor(h[:], relu[:], spread[:, first : first + PIECE], MULT)
                nc.tensor.matmul(
                    window[:].indirect(offsets[:, first // 16 : (first + PIECE) // 16]),
                    w2_sb[:, a, :],
                    h[:],
                    start=False,
                    stop=a == HB - 1 and first + PIECE == N,
                )

        for first in PIECES:
            out_sb = held.tile([P, PIECE], F32, name=f"out_{first}")
            nc.vector.tensor_copy(out_sb[:], window[:, first : first + PIECE])
            nc.sync.dma_start(out[:, first : first + PIECE], out_sb[:])
